import numpy as np, ml_dtypes
CORES = [14,30,46,142,158,174,270,286,302,398,414,430]
N = 12
KB, QP = 4, 128
MEM = [8]
def setup_inputs(rng):
    q = rng.standard_normal((N, 128, QP), dtype=np.float32) / 4; k = rng.standard_normal((N, 128, KB * 128), dtype=np.float32)
    a = 2 * np.pi * rng.random((N, QP)); s = 400 * rng.random((N, QP)) ** 1.5; q[:, 0, :] = s * np.cos(a); q[:, 1, :] = s * np.sin(a); q[:, 2, :] = 150 * rng.standard_normal((N, QP)); k[:, 2, :] = 1 + k[:, 2, :] / 50
    c = np.zeros(N); c[MEM] = rng.permutation(len(MEM))
    a = (2 * np.pi * rng.random() + np.pi / 2 * (c.reshape(N, 1, 1) + 0.5) / len(MEM) - 0.5 + (np.arange(KB).reshape(1, KB, 1) + rng.random((N, KB, 128))) / KB).reshape(N, KB * 128); k[:, 0, :] = np.cos(a); k[:, 1, :] = np.sin(a)
    return {"q": q.astype(ml_dtypes.bfloat16), "k": k.astype(ml_dtypes.bfloat16), "v": rng.standard_normal((N, 128, KB * 128), dtype=np.float32).astype(ml_dtypes.bfloat16)}
def setup_inputs_big(rng):
    d = setup_inputs(rng)
    for k in ("v",): d[k] = (d[k].astype(np.float32) * 1048576.0).astype(d[k].dtype)
    return d
def setup_inputs_small(rng):
    d = setup_inputs(rng)
    for k in ("v",): d[k] = (d[k].astype(np.float32) * (1 / 1048576.0)).astype(d[k].dtype)
    return d
def reference(q, k, v):
    Q, K, V = q.astype(np.float64), k.astype(np.float64), v.astype(np.float64)
    y = np.zeros((N, QP, 128))
    for r in range(N):
        js = list(MEM)
        S = np.concatenate([K[j].T @ Q[r] for j in js], axis=0)
        P = np.exp(S - S.max(axis=0)); P = P / P.sum(axis=0)
        y[r] = P.T @ np.concatenate([V[j][:, 128 * b:128 * b + 128] for j in js for b in range(KB)], axis=0)
    return {"y": y.astype(ml_dtypes.bfloat16)}

@@ -1,0 +1,292 @@
+from concourse.bass import DstId, RemoteDMATransfer
+from concourse.mybir import AluOpType, AxisListType, ActivationFunctionType
+
+NS = 4
+W = 128
+HALF = 256
+
+SCRATCH = {
+    "kv": ("sbuf", [128, 8 * W], "bfloat16"),
+    "qin": ("sbuf", [128, NS * W], "bfloat16"),
+    "zer": ("sbuf", [128, W], "bfloat16"),
+    "one": ("sbuf", [128, W], "bfloat16"),
+    "idn": ("sbuf", [128, W], "bfloat16"),
+    "nm": ("sbuf", [128, 2 * NS], "float32"),
+    "ng": ("sbuf", [128, NS], "float32"),
+    "sm": ("sbuf", [128, 2 * NS], "float32"),
+    "ls": ("sbuf", [128, NS], "float32"),
+    "rl": ("sbuf", [128, NS], "float32"),
+    "pw": ("sbuf", [128, NS * 4 * W], "bfloat16"),
+    "pt": ("sbuf", [128, NS * 4 * W], "bfloat16"),
+    "yo": ("sbuf", [128, NS * W], "bfloat16"),
+    "qd": ("dram", [128, W], "bfloat16"),
+    "yd": ("dram", [128, W], "bfloat16"),
+    "rqd": ("dram", [128, W], "bfloat16"),
+    "ryd": ("dram", [128, W], "bfloat16"),
+    "s00": ("psum", [128, 512], "float32"),
+    "s01": ("psum", [128, 512], "float32"),
+    "s10": ("psum", [128, 512], "float32"),
+    "s11": ("psum", [128, 512], "float32"),
+    "t0": ("psum", [128, 1024], "bfloat16"),
+    "t1": ("psum", [128, 1024], "bfloat16"),
+    "y0": ("psum", [128, 512], "float32"),
+    "y1": ("psum", [128, 512], "float32"),
+}
+_SLOT_SEMS = ["qa", "sa", "sb", "nn", "mm", "ea", "eb", "ta", "tb", "ca", "cb", "ll", "rr", "vv", "yy"]
+SEMAPHORES = ["ld", "snt", "yarr", "st", "rq", "ry", "karr", "varr", "sz", "so", "si"] + [
+    n + str(i) for n in _SLOT_SEMS for i in range(NS)]
+
+_CACHE = {}
+
+
+def _cnt(mask):
+    return bin(mask).count("1")
+
+
+def _plan(T, topo):
+    if "p" in _CACHE:
+        return _CACHE["p"]
+    cores = [int(c) for c in T.cores]
+    mem_rank = int(T.tables["MEM"][0])
+    mem = cores[mem_rank]
+    world = range((1 + max(topo.host(c) for c in cores)) * topo.CORES_PER_HOST)
+    helpers = [c for c in world if c != mem and c not in cores and topo.host(c) == topo.host(mem)
+               and topo.chip(c) == topo.chip(mem) and topo.die(c) == topo.die(mem)]
+
+    def rack(c):
+        return topo.rack(topo.host(c))
+
+    def two_way(a, b):
+        return topo.may_write(a, b) and topo.may_write(b, a)
+
+    def direct(a, b):
+        if rack(a) == rack(b):
+            return topo.same_plane(a, b) or topo.mates(a, b)
+        return topo.chip(a) == topo.chip(b)
+
+    others = [r for r in range(len(cores)) if r != mem_rank]
+    far = [r for r in others if not two_way(cores[r], mem)]
+    near = [r for r in others if r not in far]
+    near.sort(key=lambda r: (not direct(cores[r], mem), rack(cores[r]) != rack(mem), r))
+    relay, entry = {}, {}
+    for f in far:
+        cand = [r for r in near if r not in relay.values() and two_way(cores[f], cores[r])]
+        cand.sort(key=lambda r: (not (direct(cores[f], cores[r]) and direct(cores[r], mem)),
+                                 entry.get(rack(cores[r]), 0), r))
+        relay[f] = cand[0]
+        entry[rack(cores[cand[0]])] = entry.get(rack(cores[cand[0]]), 0) + 1
+    comp = [mem] + helpers
+    slots = {c: [] for c in comp}
+    slots[mem].append(mem_rank)
+    rest = list(near)
+    for j, f in enumerate(far):
+        slots[comp[j]].append(rest.pop(0))
+        slots[comp[j]].append(f)
+    for c in comp[len(far):]:
+        for _ in range(2):
+            if rest:
+                slots[c].append(rest.pop(0))
+    j = 0
+    while rest:
+        slots[comp[j % len(far)]].append(rest.pop(0))
+        j += 1
+    where = {r: (c, s) for c in comp for s, r in enumerate(slots[c])}
+    p = {"cores": cores, "mem": mem, "mem_rank": mem_rank, "helpers": helpers, "far": far, "relay": relay,
+         "slots": slots, "where": where}
+    _CACHE["p"] = p
+    return p
+
+
+def _send(g, topo, core, dst, out_ap, in_ap, rsem, lsem):
+    rid, pid = topo.addr(dst, core)
+    m = topo.mask(core, dst)
+    g.remote_dma(out_ap=out_ap, in_ap=in_ap, remote_sem=rsem, local_sem=lsem, pid=pid, routing_id=rid,
+                 dma_engine_mask=m)
+    return _cnt(m)
+
+
+def _query_rank(g, core, rank, T, topo, pl):
+    sem, cores, relay, where = T.sem, pl["cores"], pl["relay"], pl["where"]
+    sy = g.sync
+    sy.dma_start(T.qd[:], T.q[:]).then_inc(sem.ld, 16)
+    g.wait_ge(sem.ld, 16)
+    sent = 0
+    if rank in relay:
+        ysrc = cores[relay[rank]]
+        sent += _send(g, topo, core, ysrc, T.rqd[:], T.qd[:], sem.rq, sem.snt)
+    else:
+        ysrc, s = where[rank]
+        sent += _send(g, topo, core, ysrc, T.qin[:, s * W:(s + 1) * W], T.qd[:], sem["qa%d" % s], sem.snt)
+    for f in relay:
+        if relay[f] == rank:
+            fc = cores[f]
+            cc, s = where[f]
+            g.wait_ge(sem.rq, _cnt(topo.mask(fc, core)))
+            sent += _send(g, topo, core, cc, T.qin[:, s * W:(s + 1) * W], T.rqd[:], sem["qa%d" % s], sem.snt)
+            g.wait_ge(sem.ry, _cnt(topo.mask(cc, core)))
+            sent += _send(g, topo, core, fc, T.yd[:], T.ryd[:], sem.yarr, sem.snt)
+    sy.wait_ge(sem.yarr, _cnt(topo.mask(ysrc, core)))
+    sy.dma_start(T.y[:], T.yd[:]).then_inc(sem.st, 16)
+    sy.wait_ge(sem.st, 16)
+    g.wait_ge(sem.snt, sent)
+
+
+def _compute_core(g, core, T, topo, pl):
+    sem, cores, relay = T.sem, pl["cores"], pl["relay"]
+    mine = pl["slots"][core]
+    n = len(mine)
+    is_mem = core == pl["mem"]
+    pe, ve, ac, sy = g.tensor, g.vector, g.scalar, g.sync
+    sbank = [[T.s00, T.s01], [T.s10, T.s11]]
+    tbank = [T.t0, T.t1]
+    ybank = [T.y0, T.y1]
+    once = {}
+
+    def S(name, i):
+        return sem["%s%d" % (name, i)]
+
+    def first(q, key, s, val):
+        if key not in once:
+            once[key] = True
+            q.wait_ge(s, val)
+
+    qthr = []
+    for r in mine:
+        if r == pl["mem_rank"]:
+            qthr.append(16)
+        else:
+            src = cores[relay[r]] if r in relay else cores[r]
+            qthr.append(_cnt(topo.mask(src, core)))
+
+    if is_mem:
+        sy.dma_start(T.kv[:, 0:4 * W], T.k[:]).then_inc(sem.karr, 16)
+        ac.dma_start(T.kv[:, 4 * W:8 * W], T.v[:]).then_inc(sem.varr, 16)
+        sy.dma_start(T.qin[:, 0:W], T.q[:]).then_inc(S("qa", 0), 16)
+    ve.memset(T.zer[:], 0.0).then_inc(sem.sz, 1)
+    ac.wait_ge(sem.sz, 1)
+    ac.activation(T.one[:], T.zer[:], ActivationFunctionType.Exp).then_inc(sem.so, 1)
+    g.wait_ge(sem.so, 1)
+    g.affine_select(T.idn[:], T.one[:], [[-1, W]], AluOpType.is_equal, 0.0, 0, 1).then_inc(sem.si, 1)
+
+    def pe_S(i):
+        first(pe, "pk", sem.karr, 16)
+        pe.wait_ge(S("qa", i), qthr[i])
+        for h in (0, 1):
+            pe.matmul(sbank[i % 2][h][:, 0:HALF], T.qin[:, i * W:(i + 1) * W], T.kv[:, h * HALF:(h + 1) * HALF],
+                      True, True).then_inc(S("sa" if h == 0 else "sb", i), 1)
+
+    def pe_T(i, h):
+        first(pe, "pi", sem.si, 1)
+        pe.wait_ge(S("ea" if h == 0 else "eb", i), 1)
+        for b in (0, 1):
+            c = 4 * W * i + HALF * h + W * b
+            pe.transpose(tbank[h][:, b * W:(b + 1) * W], T.pw[:, c:c + W], T.idn[:]).then_inc(
+                S("ta" if h == 0 else "tb", i), 1)
+
+    def pe_PV(i, h):
+        first(pe, "pv", sem.varr, 16)
+        pe.wait_ge(S("ca" if h == 0 else "cb", i), 1)
+        if h == 0 and i >= 2:
+            pe.wait_ge(S("yy", i - 2), 1)
+        for b in (2 * h, 2 * h + 1):
+            c = 4 * W * i + W * b
+            pe.matmul(ybank[i % 2][:, 0:W], T.pt[:, c:c + W], T.kv[:, (4 + b) * W:(5 + b) * W],
+                      b == 0, b == 3).then_inc(S("vv", i), 1)
+
+    def ve_MX(i, h):
+        ve.wait_ge(S("sa" if h == 0 else "sb", i), 1)
+        ve.tensor_reduce(T.nm[:, 2 * i + h:2 * i + h + 1], sbank[i % 2][h][:, 0:HALF], AxisListType.X,
+                         AluOpType.max, negate=True).then_inc(S("nn", i), 1)
+
+    def ve_CB(i):
+        ve.wait_ge(S("nn", i), 2)
+        ve.tensor_tensor(T.ng[:, i:i + 1], T.nm[:, 2 * i:2 * i + 1], T.nm[:, 2 * i + 1:2 * i + 2],
+                         AluOpType.min).then_inc(S("mm", i), 1)
+
+    def ve_CP(i, h):
+        ve.wait_ge(S("ta" if h == 0 else "tb", i), 2)
+        c = 4 * W * i + HALF * h
+        ve.tensor_copy(T.pt[:, c:c + HALF], tbank[h][:, 0:HALF]).then_inc(S("ca" if h == 0 else "cb", i), 1)
+
+    def ve_AD(i):
+        ve.wait_ge(S("ea", i), 1)
+        ve.wait_ge(S("eb", i), 1)
+        ve.tensor_tensor(T.ls[:, i:i + 1], T.sm[:, 2 * i:2 * i + 1], T.sm[:, 2 * i + 1:2 * i + 2],
+                         AluOpType.add).then_inc(S("ll", i), 1)
+
+    def ve_RC(i):
+        ve.wait_ge(S("ll", i), 1)
+        ve.reciprocal(T.rl[:, i:i + 1], T.ls[:, i:i + 1]).then_inc(S("rr", i), 1)
+
+    def ve_SC(i):
+        ve.wait_ge(S("rr", i), 1)
+        ve.wait_ge(S("vv", i), 4)
+        ve.tensor_scalar(T.yo[:, i * W:(i + 1) * W], ybank[i % 2][:, 0:W], T.rl[:, i:i + 1], None,
+                         AluOpType.mult).then_inc(S("yy", i), 1)
+
+    def ac_EX(i):
+        ac.wait_ge(S("mm", i), 1)
+        for h in (0, 1):
+            c = 4 * W * i + HALF * h
+            ac.activation(T.pw[:, c:c + HALF], sbank[i % 2][h][:, 0:HALF], ActivationFunctionType.Exp,
+                          bias=T.ng[:, i:i + 1], scale=1.0,
+                          accum_out=T.sm[:, 2 * i + h:2 * i + h + 1]).then_inc(S("ea" if h == 0 else "eb", i), 1)
+
+    has_far = any(r in relay for r in mine)
+    i = 0
+    while i < n:
+        pair = i + 1 < n and mine[i + 1] not in relay and (mine[i] in relay or not has_far)
+        if pair:
+            j = i + 1
+            pe_S(i); pe_S(j)
+            pe_T(i, 0); pe_T(i, 1); pe_PV(i, 0); pe_PV(i, 1)
+            pe_T(j, 0); pe_T(j, 1); pe_PV(j, 0); pe_PV(j, 1)
+            ve_MX(i, 0); ve_MX(i, 1); ve_CB(i); ve_MX(j, 0); ve_MX(j, 1)
+            ve_CP(i, 0); ve_CB(j); ve_AD(i); ve_CP(i, 1); ve_RC(i); ve_SC(i)
+            ve_CP(j, 0); ve_AD(j); ve_CP(j, 1); ve_RC(j); ve_SC(j)
+            ac_EX(i); ac_EX(j)
+            i += 2
+        else:
+            pe_S(i); pe_T(i, 0); pe_T(i, 1); pe_PV(i, 0); pe_PV(i, 1)
+            ve_MX(i, 0); ve_MX(i, 1); ve_CB(i); ve_CP(i, 0); ve_AD(i); ve_CP(i, 1); ve_RC(i); ve_SC(i)
+            ac_EX(i)
+            i += 1
+
+    sent = 0
+    if is_mem and pl["helpers"]:
+        m = topo.mask(core, pl["helpers"][0])
+        for h in pl["helpers"]:
+            m &= topo.mask(core, h)
+        ids = []
+        for h in pl["helpers"]:
+            rid, pid = topo.addr(h, core)
+            ids.append(DstId(rid=rid, pnc=pid))
+        for lo, s in ((0, sem.karr), (4 * W, sem.varr)):
+            g.wait_ge(s, 16)
+            piece = T.kv[:, lo:lo + 4 * W]
+            g.remote_dma_fused([RemoteDMATransfer(dst_ids=ids, dma_engine_mask=m, remote_sem=s, srcs=[piece],
+                                                  dsts=[piece for _ in ids], alu_op=0)], local_sem=sem.snt)
+            sent += _cnt(m)
+    for i, r in enumerate(mine):
+        yo = T.yo[:, i * W:(i + 1) * W]
+        if r == pl["mem_rank"]:
+            sy.wait_ge(S("yy", i), 1)
+            sy.dma_start(T.y[:], yo).then_inc(sem.st, 16)
+            sy.wait_ge(sem.st, 16)
+            continue
+        g.wait_ge(S("yy", i), 1)
+        if r in relay:
+            sent += _send(g, topo, core, cores[relay[r]], T.ryd[:], yo, sem.ry, sem.snt)
+        else:
+            sent += _send(g, topo, core, cores[r], T.yd[:], yo, sem.yarr, sem.snt)
+    g.wait_ge(sem.snt, sent)
+
+
+def rank_program(g, core, T, topo):
+    pl = _plan(T, topo)
+    if core in pl["slots"]:
+        _compute_core(g, core, T, topo, pl)
+        return
+    rank = T.rank_of(core)
+    if rank is not None:
+        _query_rank(g, core, rank, T, topo, pl)

@@ -80,10 +80,11 @@ def _plan(T, topo):
     slots[mem].append(mem_rank)
     rest = list(near)
     for j, f in enumerate(far):
-        slots[comp[j]].append(rest.pop(0))
+        if comp[j] != mem:
+            slots[comp[j]].append(rest.pop(0))
         slots[comp[j]].append(f)
     for c in comp[len(far):]:
-        for _ in range(2):
+        for _ in range(3):
             if rest:
                 slots[c].append(rest.pop(0))
     j = 0
@@ -232,25 +233,35 @@ def _compute_core(g, core, T, topo, pl):
                           bias=T.ng[:, i:i + 1], scale=1.0,
                           accum_out=T.sm[:, 2 * i + h:2 * i + h + 1]).then_inc(S("ea" if h == 0 else "eb", i), 1)
 
-    has_far = any(r in relay for r in mine)
-    i = 0
-    while i < n:
-        pair = i + 1 < n and mine[i + 1] not in relay and (mine[i] in relay or not has_far)
-        if pair:
-            j = i + 1
-            pe_S(i); pe_S(j)
+    def run(grp):
+        m = len(grp)
+        pe_S(grp[0])
+        if m > 1:
+            pe_S(grp[1])
+        for a, i in enumerate(grp):
             pe_T(i, 0); pe_T(i, 1); pe_PV(i, 0); pe_PV(i, 1)
-            pe_T(j, 0); pe_T(j, 1); pe_PV(j, 0); pe_PV(j, 1)
-            ve_MX(i, 0); ve_MX(i, 1); ve_CB(i); ve_MX(j, 0); ve_MX(j, 1)
-            ve_CP(i, 0); ve_CB(j); ve_AD(i); ve_CP(i, 1); ve_RC(i); ve_SC(i)
-            ve_CP(j, 0); ve_AD(j); ve_CP(j, 1); ve_RC(j); ve_SC(j)
-            ac_EX(i); ac_EX(j)
-            i += 2
-        else:
-            pe_S(i); pe_T(i, 0); pe_T(i, 1); pe_PV(i, 0); pe_PV(i, 1)
-            ve_MX(i, 0); ve_MX(i, 1); ve_CB(i); ve_CP(i, 0); ve_AD(i); ve_CP(i, 1); ve_RC(i); ve_SC(i)
+            if a + 2 < m:
+                pe_S(grp[a + 2])
+        ve_MX(grp[0], 0); ve_MX(grp[0], 1); ve_CB(grp[0])
+        if m > 1:
+            ve_MX(grp[1], 0); ve_MX(grp[1], 1)
+        for a, i in enumerate(grp):
+            ve_CP(i, 0)
+            if a == 0 and m > 1:
+                ve_CB(grp[1])
+            ve_AD(i); ve_CP(i, 1); ve_RC(i); ve_SC(i)
+            if a + 2 < m:
+                k = grp[a + 2]
+                ve_MX(k, 0); ve_MX(k, 1); ve_CB(k)
+        for i in grp:
             ac_EX(i)
-            i += 1
+
+    if is_mem:
+        run([0])
+        if n > 1:
+            run(list(range(1, n)))
+    elif n:
+        run(list(range(n)))
 
     sent = 0
     if is_mem and pl["helpers"]:

from concourse.bass import DstId, RemoteDMATransfer
from concourse.mybir import AluOpType, AxisListType, ActivationFunctionType

NS = 4
W = 128
HALF = 256

SCRATCH = {
    "kv": ("sbuf", [128, 8 * W], "bfloat16"),
    "qin": ("sbuf", [128, NS * W], "bfloat16"),
    "zer": ("sbuf", [128, W], "bfloat16"),
    "one": ("sbuf", [128, W], "bfloat16"),
    "idn": ("sbuf", [128, W], "bfloat16"),
    "nm": ("sbuf", [128, 2 * NS], "float32"),
    "ng": ("sbuf", [128, NS], "float32"),
    "sm": ("sbuf", [128, 2 * NS], "float32"),
    "ls": ("sbuf", [128, NS], "float32"),
    "rl": ("sbuf", [128, NS], "float32"),
    "pw": ("sbuf", [128, NS * 4 * W], "bfloat16"),
    "pt": ("sbuf", [128, NS * 4 * W], "bfloat16"),
    "yo": ("sbuf", [128, NS * W], "bfloat16"),
    "qd": ("dram", [128, W], "bfloat16"),
    "yd": ("dram", [128, W], "bfloat16"),
    "rqd": ("dram", [128, W], "bfloat16"),
    "ryd": ("dram", [128, W], "bfloat16"),
    "s00": ("psum", [128, 512], "float32"),
    "s01": ("psum", [128, 512], "float32"),
    "s10": ("psum", [128, 512], "float32"),
    "s11": ("psum", [128, 512], "float32"),
    "t0": ("psum", [128, 1024], "bfloat16"),
    "t1": ("psum", [128, 1024], "bfloat16"),
    "y0": ("psum", [128, 512], "float32"),
    "y1": ("psum", [128, 512], "float32"),
}
_SLOT_SEMS = ["qa", "sa", "sb", "nn", "mm", "ea", "eb", "ta", "tb", "ca", "cb", "ll", "rr", "vv", "yy"]
SEMAPHORES = ["ld", "snt", "yarr", "st", "rq", "ry", "karr", "varr", "sz", "so", "si"] + [
    n + str(i) for n in _SLOT_SEMS for i in range(NS)]

_CACHE = {}


def _cnt(mask):
    return bin(mask).count("1")


def _plan(T, topo):
    if "p" in _CACHE:
        return _CACHE["p"]
    cores = [int(c) for c in T.cores]
    mem_rank = int(T.tables["MEM"][0])
    mem = cores[mem_rank]
    world = range((1 + max(topo.host(c) for c in cores)) * topo.CORES_PER_HOST)
    helpers = [c for c in world if c != mem and c not in cores and topo.host(c) == topo.host(mem)
               and topo.chip(c) == topo.chip(mem) and topo.die(c) == topo.die(mem)]

    def rack(c):
        return topo.rack(topo.host(c))

    def two_way(a, b):
        return topo.may_write(a, b) and topo.may_write(b, a)

    def direct(a, b):
        if rack(a) == rack(b):
            return topo.same_plane(a, b) or topo.mates(a, b)
        return topo.chip(a) == topo.chip(b)

    others = [r for r in range(len(cores)) if r != mem_rank]
    far = [r for r in others if not two_way(cores[r], mem)]
    near = [r for r in others if r not in far]
    near.sort(key=lambda r: (not direct(cores[r], mem), rack(cores[r]) != rack(mem), r))
    relay, entry = {}, {}
    for f in far:
        cand = [r for r in near if r not in relay.values() and two_way(cores[f], cores[r])]
        cand.sort(key=lambda r: (not (direct(cores[f], cores[r]) and direct(cores[r], mem)),
                                 entry.get(rack(cores[r]), 0), r))
        relay[f] = cand[0]
        entry[rack(cores[cand[0]])] = entry.get(rack(cores[cand[0]]), 0) + 1
    comp = [mem] + helpers
    slots = {c: [] for c in comp}
    slots[mem].append(mem_rank)
    rest = list(near)
    for j, f in enumerate(far):
        if comp[j] != mem:
            slots[comp[j]].append(rest.pop(0))
        slots[comp[j]].append(f)
    for c in comp[len(far):]:
        for _ in range(3):
            if rest:
                slots[c].append(rest.pop(0))
    j = 0
    while rest:
        slots[comp[j % len(far)]].append(rest.pop(0))
        j += 1
    where = {r: (c, s) for c in comp for s, r in enumerate(slots[c])}
    p = {"cores": cores, "mem": mem, "mem_rank": mem_rank, "helpers": helpers, "far": far, "relay": relay,
         "slots": slots, "where": where}
    _CACHE["p"] = p
    return p


def _send(g, topo, core, dst, out_ap, in_ap, rsem, lsem):
    rid, pid = topo.addr(dst, core)
    m = topo.mask(core, dst)
    g.remote_dma(out_ap=out_ap, in_ap=in_ap, remote_sem=rsem, local_sem=lsem, pid=pid, routing_id=rid,
                 dma_engine_mask=m)
    return _cnt(m)


def _query_rank(g, core, rank, T, topo, pl):
    sem, cores, relay, where = T.sem, pl["cores"], pl["relay"], pl["where"]
    sy = g.sync
    sy.dma_start(T.qd[:], T.q[:]).then_inc(sem.ld, 16)
    g.wait_ge(sem.ld, 16)
    sent = 0
    if rank in relay:
        ysrc = cores[relay[rank]]
        sent += _send(g, topo, core, ysrc, T.rqd[:], T.qd[:], sem.rq, sem.snt)
    else:
        ysrc, s = where[rank]
        sent += _send(g, topo, core, ysrc, T.qin[:, s * W:(s + 1) * W], T.qd[:], sem["qa%d" % s], sem.snt)
    for f in relay:
        if relay[f] == rank:
            fc = cores[f]
            cc, s = where[f]
            g.wait_ge(sem.rq, _cnt(topo.mask(fc, core)))
            sent += _send(g, topo, core, cc, T.qin[:, s * W:(s + 1) * W], T.rqd[:], sem["qa%d" % s], sem.snt)
            g.wait_ge(sem.ry, _cnt(topo.mask(cc, core)))
            sent += _send(g, topo, core, fc, T.yd[:], T.ryd[:], sem.yarr, sem.snt)
    sy.wait_ge(sem.yarr, _cnt(topo.mask(ysrc, core)))
    sy.dma_start(T.y[:], T.yd[:]).then_inc(sem.st, 16)
    sy.wait_ge(sem.st, 16)
    g.wait_ge(sem.snt, sent)


def _compute_core(g, core, T, topo, pl):
    sem, cores, relay = T.sem, pl["cores"], pl["relay"]
    mine = pl["slots"][core]
    n = len(mine)
    is_mem = core == pl["mem"]
    pe, ve, ac, sy = g.tensor, g.vector, g.scalar, g.sync
    sbank = [[T.s00, T.s01], [T.s10, T.s11]]
    tbank = [T.t0, T.t1]
    ybank = [T.y0, T.y1]
    once = {}

    def S(name, i):
        return sem["%s%d" % (name, i)]

    def first(q, key, s, val):
        if key not in once:
            once[key] = True
            q.wait_ge(s, val)

    qthr = []
    for r in mine:
        if r == pl["mem_rank"]:
            qthr.append(16)
        else:
            src = cores[relay[r]] if r in relay else cores[r]
            qthr.append(_cnt(topo.mask(src, core)))

    if is_mem:
        sy.dma_start(T.kv[:, 0:4 * W], T.k[:]).then_inc(sem.karr, 16)
        ac.dma_start(T.kv[:, 4 * W:8 * W], T.v[:]).then_inc(sem.varr, 16)
        sy.dma_start(T.qin[:, 0:W], T.q[:]).then_inc(S("qa", 0), 16)
    ve.memset(T.zer[:], 0.0).then_inc(sem.sz, 1)
    ac.wait_ge(sem.sz, 1)
    ac.activation(T.one[:], T.zer[:], ActivationFunctionType.Exp).then_inc(sem.so, 1)
    g.wait_ge(sem.so, 1)
    g.affine_select(T.idn[:], T.one[:], [[-1, W]], AluOpType.is_equal, 0.0, 0, 1).then_inc(sem.si, 1)

    def pe_S(i):
        first(pe, "pk", sem.karr, 16)
        pe.wait_ge(S("qa", i), qthr[i])
        for h in (0, 1):
            pe.matmul(sbank[i % 2][h][:, 0:HALF], T.qin[:, i * W:(i + 1) * W], T.kv[:, h * HALF:(h + 1) * HALF],
                      True, True).then_inc(S("sa" if h == 0 else "sb", i), 1)

    def pe_T(i, h):
        first(pe, "pi", sem.si, 1)
        pe.wait_ge(S("ea" if h == 0 else "eb", i), 1)
        for b in (0, 1):
            c = 4 * W * i + HALF * h + W * b
            pe.transpose(tbank[h][:, b * W:(b + 1) * W], T.pw[:, c:c + W], T.idn[:]).then_inc(
                S("ta" if h == 0 else "tb", i), 1)

    def pe_PV(i, h):
        first(pe, "pv", sem.varr, 16)
        pe.wait_ge(S("ca" if h == 0 else "cb", i), 1)
        if h == 0 and i >= 2:
            pe.wait_ge(S("yy", i - 2), 1)
        for b in (2 * h, 2 * h + 1):
            c = 4 * W * i + W * b
            pe.matmul(ybank[i % 2][:, 0:W], T.pt[:, c:c + W], T.kv[:, (4 + b) * W:(5 + b) * W],
                      b == 0, b == 3).then_inc(S("vv", i), 1)

    def ve_MX(i, h):
        ve.wait_ge(S("sa" if h == 0 else "sb", i), 1)
        ve.tensor_reduce(T.nm[:, 2 * i + h:2 * i + h + 1], sbank[i % 2][h][:, 0:HALF], AxisListType.X,
                         AluOpType.max, negate=True).then_inc(S("nn", i), 1)

    def ve_CB(i):
        ve.wait_ge(S("nn", i), 2)
        ve.tensor_tensor(T.ng[:, i:i + 1], T.nm[:, 2 * i:2 * i + 1], T.nm[:, 2 * i + 1:2 * i + 2],
                         AluOpType.min).then_inc(S("mm", i), 1)

    def ve_CP(i, h):
        ve.wait_ge(S("ta" if h == 0 else "tb", i), 2)
        c = 4 * W * i + HALF * h
        ve.tensor_copy(T.pt[:, c:c + HALF], tbank[h][:, 0:HALF]).then_inc(S("ca" if h == 0 else "cb", i), 1)

    def ve_AD(i):
        ve.wait_ge(S("ea", i), 1)
        ve.wait_ge(S("eb", i), 1)
        ve.tensor_tensor(T.ls[:, i:i + 1], T.sm[:, 2 * i:2 * i + 1], T.sm[:, 2 * i + 1:2 * i + 2],
                         AluOpType.add).then_inc(S("ll", i), 1)

    def ve_RC(i):
        ve.wait_ge(S("ll", i), 1)
        ve.reciprocal(T.rl[:, i:i + 1], T.ls[:, i:i + 1]).then_inc(S("rr", i), 1)

    def ve_SC(i):
        ve.wait_ge(S("rr", i), 1)
        ve.wait_ge(S("vv", i), 4)
        ve.tensor_scalar(T.yo[:, i * W:(i + 1) * W], ybank[i % 2][:, 0:W], T.rl[:, i:i + 1], None,
                         AluOpType.mult).then_inc(S("yy", i), 1)

    def ac_EX(i):
        ac.wait_ge(S("mm", i), 1)
        for h in (0, 1):
            c = 4 * W * i + HALF * h
            ac.activation(T.pw[:, c:c + HALF], sbank[i % 2][h][:, 0:HALF], ActivationFunctionType.Exp,
                          bias=T.ng[:, i:i + 1], scale=1.0,
                          accum_out=T.sm[:, 2 * i + h:2 * i + h + 1]).then_inc(S("ea" if h == 0 else "eb", i), 1)

    def run(grp):
        m = len(grp)
        pe_S(grp[0])
        if m > 1:
            pe_S(grp[1])
        for a, i in enumerate(grp):
            pe_T(i, 0); pe_T(i, 1); pe_PV(i, 0); pe_PV(i, 1)
            if a + 2 < m:
                pe_S(grp[a + 2])
        ve_MX(grp[0], 0); ve_MX(grp[0], 1); ve_CB(grp[0])
        if m > 1:
            ve_MX(grp[1], 0); ve_MX(grp[1], 1)
        for a, i in enumerate(grp):
            ve_CP(i, 0)
            if a == 0 and m > 1:
                ve_CB(grp[1])
            ve_AD(i); ve_CP(i, 1); ve_RC(i); ve_SC(i)
            if a + 2 < m:
                k = grp[a + 2]
                ve_MX(k, 0); ve_MX(k, 1); ve_CB(k)
        for i in grp:
            ac_EX(i)

    if is_mem:
        run([0])
        if n > 1:
            run(list(range(1, n)))
    elif n:
        run(list(range(n)))

    sent = 0
    if is_mem and pl["helpers"]:
        m = topo.mask(core, pl["helpers"][0])
        for h in pl["helpers"]:
            m &= topo.mask(core, h)
        ids = []
        for h in pl["helpers"]:
            rid, pid = topo.addr(h, core)
            ids.append(DstId(rid=rid, pnc=pid))
        for lo, s in ((0, sem.karr), (4 * W, sem.varr)):
            g.wait_ge(s, 16)
            piece = T.kv[:, lo:lo + 4 * W]
            g.remote_dma_fused([RemoteDMATransfer(dst_ids=ids, dma_engine_mask=m, remote_sem=s, srcs=[piece],
                                                  dsts=[piece for _ in ids], alu_op=0)], local_sem=sem.snt)
            sent += _cnt(m)
    for i, r in enumerate(mine):
        yo = T.yo[:, i * W:(i + 1) * W]
        if r == pl["mem_rank"]:
            sy.wait_ge(S("yy", i), 1)
            sy.dma_start(T.y[:], yo).then_inc(sem.st, 16)
            sy.wait_ge(sem.st, 16)
            continue
        g.wait_ge(S("yy", i), 1)
        if r in relay:
            sent += _send(g, topo, core, cores[relay[r]], T.ryd[:], yo, sem.ry, sem.snt)
        else:
            sent += _send(g, topo, core, cores[r], T.yd[:], yo, sem.yarr, sem.snt)
    g.wait_ge(sem.snt, sent)


def rank_program(g, core, T, topo):
    pl = _plan(T, topo)
    if core in pl["slots"]:
        _compute_core(g, core, T, topo, pl)
        return
    rank = T.rank_of(core)
    if rank is not None:
        _query_rank(g, core, rank, T, topo, pl)
